import numpy as np
import ml_dtypes


def mxq(x, axis, fmt="e4m3"):
    dtype, down = {"e4m3": (ml_dtypes.float8_e4m3fn, 7), "e5m2": (ml_dtypes.float8_e5m2, 14)}[fmt]
    v = np.moveaxis(np.asarray(x, np.float32).astype(ml_dtypes.bfloat16).astype(np.float64), axis, -1)
    blocks = v.reshape(v.shape[:-1] + (-1, 32))
    amax = np.abs(blocks).max(-1, keepdims=True)
    byte = np.maximum(np.where(amax > 0, np.frexp(amax)[1] - 1 + 127, 0) - down, 1)
    scale = np.exp2(byte - 127.0)
    codes = (blocks / scale).astype(np.float32).astype(dtype).astype(np.float64)
    return np.moveaxis((codes * scale).reshape(v.shape), -1, axis)


WIDE = False


def mx_kscale(k):
    if not WIDE:
        return np.ones(k)
    levels = np.array([10, -10, 5, -5, 0])
    if k % 512:
        return np.exp2(np.random.permutation(np.resize(levels, k // 32))).repeat(32)
    a = np.empty((k // 512, 16))
    for p in range(k // 512):
        a[p, :8] = np.random.permutation(np.resize(levels, 8))
        for g in range(8):
            far = levels[np.abs(levels - a[p, g]) >= 10]
            a[p, g + 8] = far[np.random.randint(len(far))]
    return np.exp2(a.ravel()).repeat(32)


BF16 = ml_dtypes.bfloat16


def bf(x):
    return np.asarray(x, np.float32).astype(BF16)


def f64(x):
    return np.asarray(x).astype(np.float64)


E2M1 = np.array([0.0, 0.5, 1.0, 1.5, 2.0, 3.0, 4.0, 6.0, -0.0, -0.5, -1.0, -1.5, -2.0, -3.0, -4.0, -6.0])


def pack_weight(w, fmt):
    k, n = w.shape
    w = f64(bf(w)).reshape(k // 32, 32, n)
    amax = np.abs(w).max(1)
    if fmt == "e4m3":
        byte = np.frexp(amax)[1] - 1 + 127 - 7
    else:
        mant, ex = np.frexp(amax / 6.0)
        byte = np.where(mant > 0.5, ex, ex - 1) + 127
    byte = np.clip(np.where(amax > 0, byte, 1), 1, 254)
    scaled = (w * np.exp2(127.0 - byte)[:, None, :]).reshape(k, n).astype(np.float32)
    by_word = np.ascontiguousarray(scaled.reshape(k // 512, 128, 4, n).transpose(0, 1, 3, 2))
    if fmt == "e4m3":
        words = by_word.astype(ml_dtypes.float8_e4m3fn).view(np.uint8)
    else:
        c = by_word.astype(ml_dtypes.float4_e2m1fn).view(np.uint8) & 0xF
        words = c[..., 0::2] | (c[..., 1::2] << 4)
    return np.ascontiguousarray(words), np.ascontiguousarray(byte.astype(np.uint8).reshape(k // 512, 16, n))


def unpack_weight(words, scales, fmt):
    g, p, n, _ = words.shape
    if fmt == "e4m3":
        vals = np.ascontiguousarray(words).view(ml_dtypes.float8_e4m3fn).astype(np.float64)
    else:
        nib = np.empty((g, p, n, 4), np.uint8)
        nib[..., 0::2] = words & 0xF
        nib[..., 1::2] = words >> 4
        vals = E2M1[nib]
    vals = vals * np.repeat(np.exp2(scales.astype(np.float64) - 127.0), 8, axis=1)[..., None]
    return vals.transpose(0, 1, 3, 2).reshape(g * 512, n)
def pack4(w):
    words, scales = pack_weight(w, "e2m1")
    return words.reshape(words.shape[0], 128, -1), scales


def unpack4(words, scales):
    return unpack_weight(words.reshape(words.shape[0], 128, -1, 2), scales, "e2m1")


def planes(Y):
    n, m = Y.shape
    b = f64(bf(Y)).reshape(n // 32, 32, m)
    amax = np.abs(b).max(1)
    byte = np.clip(np.where(amax > 0, np.frexp(amax)[1] - 1 + 127 - 7, 1), 1, 254)
    codes = (b * np.exp2(127.0 - byte)[:, None, :]).reshape(n, m).astype(np.float32).astype(ml_dtypes.float8_e4m3fn).view(np.uint8)
    words = codes.reshape(n // 512, 128, 4, m).transpose(0, 1, 3, 2)
    return np.ascontiguousarray(words), np.ascontiguousarray(byte.astype(np.uint8).reshape(n // 512, 16, m))


D, P, C, F, N = 3, 512, 512, 1024, 1024
EPS = 0.1
STEP = 0.35


def setup_inputs():
    s, t = mx_kscale(C), mx_kscale(F)
    x = np.random.randn(D, P, C) * s
    w_mix = STEP * np.random.randn(C, C) / np.sqrt(C) / s[:, None] * s[None, :]
    w_feat = np.random.randn(C, F) / np.sqrt(C) / s[:, None] * t[None, :]
    w_dir = np.random.randn(C, F) / np.sqrt(C) / s[:, None]
    spread = np.exp(0.8 * np.random.randn(N))
    w_out = np.random.randn(F, N) / np.sqrt(F) / t[:, None] * spread[None, :]
    w_dir_words, w_dir_scales = pack4(w_dir)
    return {"x": bf(x), "w_mix": bf(w_mix), "w_feat": bf(w_feat),
            "w_dir_words": w_dir_words, "w_dir_scales": w_dir_scales, "w_out": bf(w_out)}


def reference(x, w_mix, w_feat, w_dir_words, w_dir_scales, w_out):
    x2 = f64(x).reshape(D * P, C)
    u = x2 + (mxq(x2, 1) @ mxq(f64(w_mix), 0))
    uq = mxq(u, 1)
    a = (uq @ mxq(f64(w_feat), 0)).reshape(D, P, F)
    v = (uq @ unpack4(w_dir_words, w_dir_scales)).reshape(D, P, F)
    c = np.minimum(np.sum(a * v, axis=0), 0.0) / (np.sum(v * v, axis=0) + EPS)
    h = a - c * v
    y = (mxq(h.reshape(D * P, F), 1) @ mxq(f64(w_out), 0)).reshape(D, P, N)
    Y = y.reshape(D * P, N).T
    words, scales = planes(Y)
    return y, words, scales

@@ -1,0 +1,475 @@
+from contextlib import ExitStack
+
+import concourse.mybir as mybir
+from concourse.masks import make_identity
+
+F32 = mybir.dt.float32
+BF16 = mybir.dt.bfloat16
+I32 = mybir.dt.int32
+U32 = mybir.dt.uint32
+U8 = mybir.dt.uint8
+FP8X4 = mybir.dt.float8_e4m3fn_x4
+FP4X4 = mybir.dt.float4_e2m1fn_x4
+ALU = mybir.AluOpType
+ACT = mybir.ActivationFunctionType
+
+D, PTS, C, F, N = 3, 512, 512, 1024, 1024
+EPS = 0.1
+P = 128
+NB = PTS // P
+NG = F // 512
+FLOPS = 2 * D * PTS * (C * C + 2 * C * F + F * N)
+CONV = "G"
+YQ = ((), (), (0, 1), (1,), (0, 1), (1,), (0, 1, 2))
+NORM_LAST = False
+WO = "GGGGSSSS"
+QADD = 0
+MIXAT = (2, 4, 6)
+WOAT = (0, 1, 2, 5)
+MIXG = 4
+TC = "GG"
+TE = "VSSSSSS"
+QH_EARLY = False
+
+
+def tile_vector_neuron_relu_k1_kernel(tc, x, w_mix, w_feat, w_dir_words, w_dir_scales, w_out, out_0, out_1, out_2):
+    nc = tc.nc
+    with ExitStack() as ctx:
+        keep = ctx.enter_context(tc.tile_pool(name="keep", bufs=1))
+        work = ctx.enter_context(tc.tile_pool(name="work", bufs=2))
+        psum = ctx.enter_context(tc.psum_pool(name="psum", bufs=1))
+        ctx.enter_context(tc.manual_schedule())
+
+        taken = []
+
+        def next_bank():
+            bank = psum.tile([P, 512], F32, name="bank%d" % (len(taken) % 8))
+            taken.append(bank)
+            return bank
+
+        def mx_pair(name, width, pool=keep, bufs=None):
+            codes = pool.tile([P, width], U32, name=name + "_codes", align_bytes=64, bufs=bufs)
+            scales = pool.tile([P, width], U8, name=name + "_scales", align_bytes=64, bufs=bufs)
+            return codes, scales
+
+        def quantize(pair, cols, src):
+            nc.vector.quantize_mx(out=pair[0][:, cols].bitcast(FP8X4), scales=pair[1][:, cols], in_=src)
+
+        def mm(out, lhs, rhs, start=True, stop=True):
+            nc.tensor.matmul_mx(out=out, lhsT=lhs[0], lhsT_scale=lhs[1], rhs=rhs[0], rhs_scale=rhs[1], start=start, stop=stop)
+
+        def fp8(pair, lo, hi):
+            return pair[0][:, lo:hi].bitcast(FP8X4), pair[1][:, lo:hi]
+
+        def fp4(pair, lo, hi):
+            return pair[0][:, 2 * lo : 2 * hi].bitcast(FP4X4), pair[1][:, lo:hi]
+
+        ident = keep.tile([P, P], F32, name="ident")
+        wd_sraw = keep.tile([P, F], U8, name="wd_sraw", align_bytes=64)
+        make_identity(nc, ident[:])
+        nc.gpsimd.memset(wd_sraw[:].bitcast(I32), 0)
+        warm = keep.tile([P, 8], F32, name="warm")
+        nc.scalar.activation(out=warm[:, 0:1], in_=ident[:, 0:1], func=ACT.Abs_reciprocal_sqrt, bias=EPS)
+
+        x_sb = [keep.tile([P, D, C], BF16, name="x%d" % b, align_bytes=64) for b in range(NB)]
+        wm_raw = keep.tile([P, 4, C], BF16, name="wm_raw")
+        wf_raw = [keep.tile([P, 4, 512], BF16, name="wf_raw%d" % g) for g in range(NG)]
+        wo_raw = [keep.tile([P, 4, N], BF16, name="wo_raw%d" % g) for g in range(NG)]
+        wd_wraw = keep.tile([P, 2 * F], U8, name="wd_wraw", align_bytes=64)
+
+        def load_x(b):
+            nc.sync.dma_start(out=x_sb[b][:], in_=x[:, P * b : P * (b + 1), :].rearrange("j p c -> p j c"))
+
+        def load_wf(g):
+            nc.sync.dma_start(out=wf_raw[g][:], in_=w_feat[:, 512 * g : 512 * (g + 1)].rearrange("(p j) n -> p j n", j=4))
+
+        def load_wo(g):
+            rows = w_out.rearrange("(g s t r) n -> g r s t n", g=NG, t=4, r=4)
+            for r in range(4):
+                nc.sync.dma_start(out=wo_raw[g][r:P:4, :, :], in_=rows[g, r])
+
+        nc.sync.dma_start(out=wm_raw[:], in_=w_mix.rearrange("(p j) n -> p j n", j=4))
+        load_x(0)
+        load_x(1)
+        load_wf(0)
+        nc.sync.dma_start(out=wd_wraw[:].bitcast(I32), in_=w_dir_words[0].bitcast(I32))
+        for q in range(4):
+            nc.sync.dma_start(out=wd_sraw[32 * q : 32 * q + 4, :].bitcast(I32), in_=w_dir_scales[0, 4 * q : 4 * q + 4, :].bitcast(I32))
+        load_wf(1)
+        load_wo(0)
+        load_wo(1)
+        load_x(2)
+        load_x(3)
+
+        wm = mx_pair("wm", C)
+        wf = [mx_pair("wf%d" % g, 512) for g in range(NG)]
+        wo = [mx_pair("wo%d" % g, N) for g in range(NG)]
+        wd = (keep.tile([P, 2 * F], U8, name="wd_codes", align_bytes=64), keep.tile([P, F], U8, name="wd_scales", align_bytes=64))
+        grouped = {}
+
+        def group_wm():
+            t = work.tile([P, 2048], BF16, name="wgroup", bufs=4, align_bytes=64)
+            nc.vector.tensor_copy(
+                out=t[:].rearrange("p (t a e j) -> p a t e j", t=4, e=2, j=4),
+                in_=wm_raw[:].rearrange("p j (a e t) -> p a t e j", e=2, t=4),
+            )
+            grouped["wm"] = t
+
+        def group_wf(g):
+            if g == 1:
+                t = work.tile([P, 2048], BF16, name="wgate", bufs=1, align_bytes=64)
+            else:
+                t = work.tile([P, 2048], BF16, name="wgroup", bufs=4, align_bytes=64)
+            move = nc.scalar.copy if g == 0 else nc.vector.tensor_copy
+            move(
+                out=t[:].rearrange("p (t s r j) -> p s t j r", t=4, r=4, j=4),
+                in_=wf_raw[g][:].rearrange("p j (s t r) -> p s t j r", t=4, r=4),
+            )
+            grouped["wf", g] = t
+
+        def group_wo(g, q):
+            if q % 2 == 0 and WO[4 * g + q] == "G":
+                grouped["wo", g, q // 2] = work.tile([P, 2048], BF16, name="wgate", bufs=1, align_bytes=64)
+            elif q % 2 == 0:
+                grouped["wo", g, q // 2] = work.tile([P, 2048], BF16, name="wgroup", bufs=4, align_bytes=64)
+            t = grouped["wo", g, q // 2]
+            eng = WO[4 * g + q]
+            if eng == "G":
+                for e in range(2):
+                    lo = 1024 * (q % 2) + 512 * e
+                    nc.gpsimd.tensor_scalar(
+                        out=t[:, lo : lo + 512].rearrange("p (c i t) -> p c t i", i=4, t=4),
+                        in0=wo_raw[g][:, :, 256 * q + 128 * e : 256 * q + 128 * (e + 1)].rearrange("p t (c i) -> p c t i", i=4),
+                        scalar1=1.0, scalar2=0.0, op0=ALU.mult, op1=ALU.add,
+                    )
+            else:
+                move = nc.scalar.copy if eng == "S" else nc.vector.tensor_copy
+                move(
+                    out=t[:, 1024 * (q % 2) : 1024 * (q % 2 + 1)].rearrange("p (c i t) -> p c t i", i=4, t=4),
+                    in_=wo_raw[g][:, :, 256 * q : 256 * (q + 1)].rearrange("p t (c i) -> p c t i", i=4),
+                )
+
+        def quant_wo(g, h):
+            quantize(wo[g], slice(512 * h, 512 * (h + 1)), grouped["wo", g, h][:])
+
+        def permute_wd():
+            nc.vector.tensor_copy(
+                out=wd[0][:].bitcast(I32).rearrange("p (g t s h) -> p g t s h", g=NG, t=4, h=2),
+                in_=wd_wraw[:].bitcast(I32).rearrange("p (g s t h) -> p g t s h", g=NG, t=4, h=2),
+            )
+            nc.vector.tensor_copy(
+                out=wd[1][:].bitcast(I32).rearrange("p (g t s) -> p g t s", g=NG, t=4),
+                in_=wd_sraw[:].bitcast(I32).rearrange("p (g s t) -> p g t s", g=NG, t=4),
+            )
+
+        xt, xq, ub = {}, {}, {}
+        uq = [mx_pair("u%d" % b, D * P) for b in range(NB)]
+
+        def turn_x(b):
+            xt[b] = work.tile([P, D, P, 4], BF16, name="xt", bufs=3, align_bytes=64)
+            words = x_sb[b][:].bitcast(F32)
+            for js in ((0, 1), (2,)):
+                bank = next_bank()
+                for i, j in enumerate(js):
+                    for u in range(2):
+                        nc.tensor.transpose(bank[:, P * (2 * i + u) : P * (2 * i + u + 1)], words[:, j, u:256:2], ident[:])
+                nc.scalar.copy(
+                    out=xt[b][:, js[0] : js[-1] + 1].rearrange("p j n t -> p (j n t)").bitcast(F32).rearrange("p (j n u) -> p j n u", n=P, u=2),
+                    in_=bank[:, : 256 * len(js)].rearrange("p (j u n) -> p j n u", u=2, n=P),
+                )
+
+        def quant_x(b):
+            xq[b] = mx_pair("xq", D * P, work)
+            flat = xt[b][:].rearrange("p j n t -> p (j n t)")
+            quantize(xq[b], slice(0, 256), flat[:, 0:1024])
+            quantize(xq[b], slice(256, 384), flat[:, 1024:1536])
+
+        def mix(b, j):
+            if j == 0:
+                ub[b] = work.tile([P, D, P, 4], BF16, name="ub", align_bytes=64)
+            bank = next_bank()
+            for t in range(4):
+                mm(bank[:, P * t : P * (t + 1)], fp8(wm, P * t, P * (t + 1)), fp8(xq[b], P * j, P * (j + 1)))
+            if b >= MIXG:
+                part = work.tile([P, P, 4], F32, name="part", bufs=3)
+                nc.scalar.copy(out=part[:], in_=bank[:].rearrange("p (t n) -> p n t", t=4))
+                nc.gpsimd.tensor_tensor(out=ub[b][:, j], in0=part[:], in1=xt[b][:, j], op=ALU.add)
+            else:
+                nc.vector.tensor_tensor(out=ub[b][:, j], in0=bank[:].rearrange("p (t n) -> p n t", t=4), in1=xt[b][:, j], op=ALU.add)
+
+        def quant_u(b, j):
+            quantize(uq[b], slice(P * j, P * (j + 1)), ub[b][:, j].rearrange("p n t -> p (n t)"))
+
+        vs, sq, pr, rr, cc, mv, hb = {}, {}, {}, {}, {}, {}, {}
+        hq = {}
+
+        def dirs(k, j):
+            b, g = divmod(k, NG)
+            bank = next_bank()
+            mm(bank[:], fp8(uq[b], P * j, P * (j + 1)), fp4(wd, 512 * g, 512 * (g + 1)))
+            vs[k, j] = work.tile([P, 512], F32, name="vs", bufs=3)
+            sq[k, j] = work.tile([P, 512], F32, name="sq", bufs=4)
+            nc.scalar.copy(out=vs[k, j][:], in_=bank[:])
+            nc.scalar.activation(out=sq[k, j][:], in_=bank[:], func=ACT.Square)
+            if j >= 1 and j <= QADD:
+                nc.gpsimd.tensor_tensor(out=sq[k, j][:], in0=sq[k, j][:], in1=sq[k, j - 1][:], op=ALU.add)
+
+        def prods(k, j):
+            b, g = divmod(k, NG)
+            bank = next_bank()
+            mm(bank[:], fp8(uq[b], P * j, P * (j + 1)), fp8(wf[g], 0, 512))
+            pr[k, j] = work.tile([P, 512], F32, name="pr", bufs=4)
+            nc.vector.tensor_tensor(out=pr[k, j][:], in0=bank[:], in1=vs[k, j][:], op=ALU.mult)
+
+        def sum_turned(terms):
+            bank = next_bank()
+            for t in range(4):
+                for j in range(len(terms)):
+                    nc.tensor.matmul(bank[:, P * t : P * (t + 1)], terms[j][:, P * t : P * (t + 1)], ident[:], start=(j == 0), stop=(j == len(terms) - 1), is_transpose=True)
+            return bank[:].rearrange("p (t n) -> p n t", t=4)
+
+        def norm(k):
+            total = sum_turned([sq[k, j] for j in range(QADD, D)])
+            root = work.tile([P, P, 4], F32, name="root")
+            rr[k] = work.tile([P, P, 4], F32, name="rr")
+            nc.scalar.activation(out=root[:], in_=total, func=ACT.Abs_reciprocal_sqrt, bias=EPS)
+            nc.scalar.activation(out=rr[k][:], in_=root[:], func=ACT.Square)
+
+        def dot_sum(k):
+            return sum_turned([pr[k, j] for j in range(D)])
+
+        def coef(k, total):
+            cc[k] = work.tile([P, P, 4], F32, name="cc")
+            nc.vector.scalar_tensor_tensor(out=cc[k][:], in0=total, scalar=0.0, in1=rr[k][:], op0=ALU.min, op1=ALU.mult)
+
+        def along(k, j):
+            b, g = divmod(k, NG)
+            bank = next_bank()
+            for t in range(4):
+                mm(bank[:, P * t : P * (t + 1)], fp4(wd, 512 * g + P * t, 512 * g + P * (t + 1)), fp8(uq[b], P * j, P * (j + 1)))
+            mv[k, j] = work.tile([P, P, 4], F32, name="mv", bufs=3)
+            nc.vector.tensor_tensor(out=mv[k, j][:], in0=bank[:].rearrange("p (t n) -> p n t", t=4), in1=cc[k][:], op=ALU.mult)
+
+        def hidden(k, j):
+            b, g = divmod(k, NG)
+            bank = next_bank()
+            for t in range(4):
+                mm(bank[:, P * t : P * (t + 1)], fp8(wf[g], P * t, P * (t + 1)), fp8(uq[b], P * j, P * (j + 1)))
+            hb[k, j] = work.tile([P, P, 4], BF16, name="hb", bufs=4, align_bytes=64)
+            nc.vector.tensor_tensor(out=hb[k, j][:], in0=bank[:].rearrange("p (t n) -> p n t", t=4), in1=mv[k, j][:], op=ALU.subtract)
+
+        def quant_h(k, j):
+            hq[k, j] = mx_pair("hq", P, work, bufs=12)
+            quantize(hq[k, j], slice(0, P), hb[k, j][:].rearrange("p n t -> p (n t)"))
+
+        ys, yb, yt = {}, {}, {}
+        y_scales = keep.tile([P, NG, D * PTS], U8, name="y_scales", align_bytes=64)
+
+        def outs(b, j, h, eng="S"):
+            if h == 0:
+                ys[b, j] = work.tile([P, N], F32, name="ys", bufs=3)
+                yb[b, j] = work.tile([P, N], BF16, name="yb", bufs=4)
+            bank = next_bank()
+            for g in range(NG):
+                mm(bank[:], fp8(hq[NG * b + g, j], 0, P), fp8(wo[g], 512 * h, 512 * (h + 1)), start=(g == 0), stop=(g == NG - 1))
+            if eng == "S":
+                nc.scalar.copy(out=ys[b, j][:, 512 * h : 512 * (h + 1)], in_=bank[:])
+            else:
+                nc.vector.tensor_copy(out=ys[b, j][:, 512 * h : 512 * (h + 1)], in_=bank[:])
+            if CONV == "S":
+                nc.scalar.copy(
+                    out=yb[b, j][:, 512 * h : 512 * (h + 1)].rearrange("n (u p e) -> n u p e", u=2, e=2),
+                    in_=bank[:].rearrange("n (p u e) -> n u p e", u=2, e=2),
+                )
+            if b == NB - 1:
+                nc.sync.dma_start(out=out_0[j, P * b : P * (b + 1), 512 * h : 512 * (h + 1)], in_=ys[b, j][:, 512 * h : 512 * (h + 1)])
+            elif h == 1:
+                nc.sync.dma_start(out=out_0[j, P * b : P * (b + 1), :], in_=ys[b, j][:])
+
+        def round_y(b, j, h, CONV=CONV):
+            dst = yb[b, j][:, 512 * h : 512 * (h + 1)].rearrange("n (u p e) -> n p u e", u=2, e=2)
+            src = ys[b, j][:, 512 * h : 512 * (h + 1)].rearrange("n (p u e) -> n p u e", u=2, e=2)
+            if CONV == "V":
+                nc.vector.tensor_copy(out=dst, in_=src)
+            if CONV == "G":
+                nc.gpsimd.tensor_scalar(out=dst, in0=src, scalar1=1.0, scalar2=0.0, op0=ALU.mult, op1=ALU.add)
+
+        def turn_y(b, j, eng="S"):
+            bank = next_bank()
+            words = yb[b, j][:].bitcast(F32)
+            for i in range(4):
+                nc.tensor.transpose(bank[:, P * i : P * (i + 1)], words[:, P * i : P * (i + 1)], ident[:])
+            yt[b, j] = work.tile([P, NG * 512], BF16, name="yt", bufs=4, align_bytes=64)
+            move = nc.scalar.copy if eng == "S" else nc.vector.tensor_copy
+            move(
+                out=yt[b, j][:].bitcast(F32).rearrange("p (g n u) -> p g n u", g=NG, u=2),
+                in_=bank[:].rearrange("p (g u n) -> p g n u", g=NG, u=2),
+            )
+
+        def quant_y(b, j):
+            cols = slice(PTS * j + P * b, PTS * j + P * (b + 1))
+            y_codes = work.tile([P, NG, P], U32, name="y_codes", bufs=6, align_bytes=64)
+            for g in range(NG):
+                nc.vector.quantize_mx(out=y_codes[:, g, :].bitcast(FP8X4), scales=y_scales[:, g, cols], in_=yt[b, j][:, 512 * g : 512 * (g + 1)])
+            dst = out_1.rearrange("g p m t -> p g (m t)").bitcast(I32)
+            nc.sync.dma_start(out=dst[:, :, cols], in_=y_codes[:].bitcast(I32))
+
+        def store_scales():
+            for q in range(4):
+                queue = nc.sync if q % 2 == 0 else nc.scalar
+                queue.dma_start(
+                    out=out_2[:, 4 * q : 4 * q + 4, :].rearrange("g r m -> r g m").bitcast(I32),
+                    in_=y_scales[32 * q : 32 * q + 4, :, :].bitcast(I32),
+                )
+
+        NK = NB * NG
+        group_wm()
+        turn_x(0)
+        turn_x(1)
+        quantize(wm, slice(0, C), grouped["wm"][:])
+        quant_x(0)
+        group_wf(0)
+        permute_wd()
+        quant_x(1)
+        mix(0, 0)
+        mix(0, 1)
+        quant_u(0, 0)
+        mix(0, 2)
+        quant_u(0, 1)
+        quantize(wf[0], slice(0, 512), grouped["wf", 0][:])
+        quant_u(0, 2)
+        group_wf(1)
+        wo_jobs = [(0, 0), (0, 1), (1, 0), (1, 1), (0, 2), (0, 3), (1, 2), (1, 3)]
+        wo_quants, rows, rounds, turns, quants = [], [], [], [], []
+
+        def skip(*args):
+            return None
+
+        def wo_step():
+            if wo_jobs:
+                job = wo_jobs.pop(0)
+                group_wo(*job)
+                if job[1] % 2 == 1:
+                    wo_quants.append((job[0], job[1] // 2))
+
+        for j in range(D):
+            dirs(0, j)
+            prods(0, j)
+            if j == 0:
+                quantize(wf[1], slice(0, 512), grouped["wf", 1][:])
+        dirs(1, 0)
+        for j in range(D):
+            mix(1, j)
+        for j in range(D):
+            quant_u(1, j)
+
+        def side(k, i):
+            if i in YQ[k] and rows:
+                b, j = rows.pop(0)
+                for h in range(2):
+                    outs(b, j, h)
+                    if CONV == "G":
+                        round_y(b, j, h)
+                rounds.append((b, j))
+            if k % 2 == 1 and (k + 3) // 2 < NB and i in MIXAT:
+                mix((k + 3) // 2, MIXAT.index(i))
+            if i in WOAT:
+                wo_step()
+
+        def window(k):
+            quant_h(k, 0) if not (QH_EARLY and not (k % 2 == 1 and (k + 3) // 2 < NB)) else None
+            quant_h(k, 1)
+            while quants:
+                quant_y(*quants.pop(0))
+            if k % 2 == 1 and (k + 3) // 2 < NB:
+                for j in range(D):
+                    quant_u((k + 3) // 2, j)
+            quant_h(k, 2)
+            if k % 2 == 1:
+                rows.extend((k // 2, j) for j in range(D))
+            if k % 2 == 0 and k // 2 + 2 < NB:
+                quant_x(k // 2 + 2)
+            while wo_quants:
+                quant_wo(*wo_quants.pop(0))
+            while rounds:
+                b, j = rounds.pop(0)
+                if CONV == "V":
+                    round_y(b, j, 0)
+                    round_y(b, j, 1)
+                turns.append((b, j))
+
+        for k in range(NK - 1):
+            first_a, first_p = dirs, prods
+            if not NORM_LAST:
+                norm(k)
+            while turns:
+                job = turns.pop(0)
+                turn_y(*job)
+                quants.append(job)
+            if k % 2 == 0 and k // 2 + 2 < NB:
+                turn_x(k // 2 + 2)
+            if NORM_LAST:
+                norm(k)
+            coef(k, dot_sum(k))
+            first_p(k + 1, 0)
+            side(k, 0)
+            along(k, 0)
+            first_a(k + 1, 1)
+            first_p(k + 1, 1)
+            hidden(k, 0)
+            side(k, 1)
+            along(k, 1)
+            first_a(k + 1, 2)
+            first_p(k + 1, 2)
+            side(k, 2)
+            hidden(k, 1)
+            side(k, 3)
+            along(k, 2)
+            side(k, 4)
+            quant_h(k, 0) if QH_EARLY and not (k % 2 == 1 and (k + 3) // 2 < NB) else None
+            side(k, 6)
+            hidden(k, 2)
+            if k + 2 < NK:
+                dirs(k + 2, 0)
+            side(k, 5)
+            window(k)
+        k = NK - 1
+        b = NB - 1
+        norm(k)
+        for job in turns:
+            turn_y(*job)
+        coef(k, dot_sum(k))
+        for job in turns[:1]:
+            quant_y(*job)
+        along(k, 0)
+        along(k, 1)
+        hidden(k, 0)
+        along(k, 2)
+        quant_h(k, 0)
+        hidden(k, 1)
+        for job in turns[1:2]:
+            quant_y(*job)
+        hidden(k, 2)
+        quant_h(k, 1)
+        outs(b, 0, 0)
+        outs(b, 0, 1)
+        for job in turns[2:]:
+            quant_y(*job)
+        quant_h(k, 2)
+        outs(b, 1, 0, TE[0])
+        round_y(b, 0, 0, "V")
+        outs(b, 1, 1, TE[1])
+        round_y(b, 0, 1, "V")
+        outs(b, 2, 0, TE[2])
+        outs(b, 2, 1, TE[3])
+        turn_y(b, 0, TE[4])
+        round_y(b, 1, 0, "V")
+        round_y(b, 1, 1, "V")
+        turn_y(b, 1, TE[5])
+        round_y(b, 2, 0, "V")
+        round_y(b, 2, 1, "V")
+        quant_y(b, 0)
+        turn_y(b, 2, TE[6])
+        quant_y(b, 1)
+        quant_y(b, 2)
+        store_scales()

@@ -20,7 +20,7 @@ NB = PTS // P
 NG = F // 512
 FLOPS = 2 * D * PTS * (C * C + 2 * C * F + F * N)
 CONV = "G"
-YQ = ((), (), (0, 1), (1,), (0, 1), (1,), (0, 1, 2))
+YQ = (0, 0, 2, 1, 2, 1, 3)
 NORM_LAST = False
 WO = "GGGGSSSS"
 QADD = 0
@@ -30,6 +30,16 @@ MIXG = 4
 TC = "GG"
 TE = "VSSSSSS"
 QH_EARLY = False
+WARM = (0, 0)
+WARMS = True
+WMV = 4
+WFV = (0, 4)
+LOADS = "m x0 x1 f0 d s f1 o0 o1 x2 x3"
+HEAD = "wp0 gm tx0 wp1 qm qx0 qx1 qx2 tx1 gf0 pw qX mx0 mx1 qu0 mx2 qu1 qf0 qu2 gf1 di0 pr0 qf1 di1 pr1 di2 pr2 dI mX0 mX1 mX2 qU0 qU1 qU2"
+TAIL = "N t0 t1 t2 C q0 m0 m1 h0 m2 H0 h1 q1 h2 H1 o00S o01S q2 H2 o10V r00V o11S r01V o20S o21S T0S r10V r11V T1S r20V r21V Q0 T2S Q1 Q2"
+MIXE = "VVVVVVVVVVVV"
+CG = "VVVVVVVV"
+ROUND = ("N T X C p0 y0 w w m0 d1 p1 h0 y1 m1 d2 p2 y2 w m2 h1 h2 D w H0 H1 q H2 x W", "N T X C p0 w w m0 d1 p1 h0 y0 m1 d2 p2 w M0 m2 h1 M1 M2 h2 D w H0 H1 q u H2 W")
 
 
 def tile_vector_neuron_relu_k1_kernel(tc, x, w_mix, w_feat, w_dir_words, w_dir_scales, w_out, out_0, out_1, out_2):
@@ -68,8 +78,12 @@ def tile_vector_neuron_relu_k1_kernel(tc, x, w_mix, w_feat, w_dir_words, w_dir_s
         wd_sraw = keep.tile([P, F], U8, name="wd_sraw", align_bytes=64)
         make_identity(nc, ident[:])
         nc.gpsimd.memset(wd_sraw[:].bitcast(I32), 0)
-        warm = keep.tile([P, 8], F32, name="warm")
-        nc.scalar.activation(out=warm[:, 0:1], in_=ident[:, 0:1], func=ACT.Abs_reciprocal_sqrt, bias=EPS)
+        if WARM[0]:
+            ones = keep.tile([P, 512], BF16, name="ones")
+            nc.vector.memset(ones[:], 1.0)
+        if WARMS:
+            warm = keep.tile([P, 8], F32, name="warm")
+            nc.scalar.activation(out=warm[:, 0:1], in_=ident[:, 0:1], func=ACT.Abs_reciprocal_sqrt, bias=EPS)
 
         x_sb = [keep.tile([P, D, C], BF16, name="x%d" % b, align_bytes=64) for b in range(NB)]
         wm_raw = keep.tile([P, 4, C], BF16, name="wm_raw")
@@ -88,18 +102,29 @@ def tile_vector_neuron_relu_k1_kernel(tc, x, w_mix, w_feat, w_dir_words, w_dir_s
             for r in range(4):
                 nc.sync.dma_start(out=wo_raw[g][r:P:4, :, :], in_=rows[g, r])
 
-        nc.sync.dma_start(out=wm_raw[:], in_=w_mix.rearrange("(p j) n -> p j n", j=4))
-        load_x(0)
-        load_x(1)
-        load_wf(0)
-        nc.sync.dma_start(out=wd_wraw[:].bitcast(I32), in_=w_dir_words[0].bitcast(I32))
-        for q in range(4):
-            nc.sync.dma_start(out=wd_sraw[32 * q : 32 * q + 4, :].bitcast(I32), in_=w_dir_scales[0, 4 * q : 4 * q + 4, :].bitcast(I32))
-        load_wf(1)
-        load_wo(0)
-        load_wo(1)
-        load_x(2)
-        load_x(3)
+        def load(tok):
+            if tok == "m":
+                nc.sync.dma_start(out=wm_raw[:], in_=w_mix.rearrange("(p j) n -> p j n", j=4))
+            if tok == "d":
+                nc.sync.dma_start(out=wd_wraw[:].bitcast(I32), in_=w_dir_words[0].bitcast(I32))
+            if tok == "s":
+                for q in range(4):
+                    nc.sync.dma_start(out=wd_sraw[32 * q : 32 * q + 4, :].bitcast(I32), in_=w_dir_scales[0, 4 * q : 4 * q + 4, :].bitcast(I32))
+            if tok[0] == "x":
+                load_x(int(tok[1]))
+            if tok[0] == "f":
+                load_wf(int(tok[1]))
+            if tok[0] == "o":
+                load_wo(int(tok[1]))
+
+        for tok in LOADS.split():
+            load(tok)
+
+        def warm_pe(n):
+            if n:
+                bank = next_bank()
+                for i in range(n):
+                    nc.tensor.matmul(bank[:], ones[:, 0:P], ones[:], start=True, stop=True)
 
         wm = mx_pair("wm", C)
         wf = [mx_pair("wf%d" % g, 512) for g in range(NG)]
@@ -109,10 +134,11 @@ def tile_vector_neuron_relu_k1_kernel(tc, x, w_mix, w_feat, w_dir_words, w_dir_s
 
         def group_wm():
             t = work.tile([P, 2048], BF16, name="wgroup", bufs=4, align_bytes=64)
-            nc.vector.tensor_copy(
-                out=t[:].rearrange("p (t a e j) -> p a t e j", t=4, e=2, j=4),
-                in_=wm_raw[:].rearrange("p j (a e t) -> p a t e j", e=2, t=4),
-            )
+            dst = t[:].rearrange("p (t a e j) -> p a t e j", t=4, e=2, j=4)
+            src = wm_raw[:].rearrange("p j (a e t) -> p a t e j", e=2, t=4)
+            nc.vector.tensor_copy(out=dst[:, :, :WMV], in_=src[:, :, :WMV])
+            if WMV < 4:
+                nc.scalar.copy(out=dst[:, :, WMV:], in_=src[:, :, WMV:])
             grouped["wm"] = t
 
         def group_wf(g):
@@ -120,11 +146,12 @@ def tile_vector_neuron_relu_k1_kernel(tc, x, w_mix, w_feat, w_dir_words, w_dir_s
                 t = work.tile([P, 2048], BF16, name="wgate", bufs=1, align_bytes=64)
             else:
                 t = work.tile([P, 2048], BF16, name="wgroup", bufs=4, align_bytes=64)
-            move = nc.scalar.copy if g == 0 else nc.vector.tensor_copy
-            move(
-                out=t[:].rearrange("p (t s r j) -> p s t j r", t=4, r=4, j=4),
-                in_=wf_raw[g][:].rearrange("p j (s t r) -> p s t j r", t=4, r=4),
-            )
+            dst = t[:].rearrange("p (t s r j) -> p s t j r", t=4, r=4, j=4)
+            src = wf_raw[g][:].rearrange("p j (s t r) -> p s t j r", t=4, r=4)
+            if WFV[g] > 0:
+                nc.vector.tensor_copy(out=dst[:, :, : WFV[g]], in_=src[:, :, : WFV[g]])
+            if WFV[g] < 4:
+                nc.scalar.copy(out=dst[:, :, WFV[g] :], in_=src[:, :, WFV[g] :])
             grouped["wf", g] = t
 
         def group_wo(g, q):
@@ -138,8 +165,8 @@ def tile_vector_neuron_relu_k1_kernel(tc, x, w_mix, w_feat, w_dir_words, w_dir_s
                 for e in range(2):
                     lo = 1024 * (q % 2) + 512 * e
                     nc.gpsimd.tensor_scalar(
-                        out=t[:, lo : lo + 512].rearrange("p (c i t) -> p c t i", i=4, t=4),
-                        in0=wo_raw[g][:, :, 256 * q + 128 * e : 256 * q + 128 * (e + 1)].rearrange("p t (c i) -> p c t i", i=4),
+                        out=t[:, lo : lo + 512].rearrange("p (n t) -> p n t", t=4),
+                        in0=wo_raw[g][:, :, 256 * q + 128 * e : 256 * q + 128 * (e + 1)].rearrange("p t n -> p n t"),
                         scalar1=1.0, scalar2=0.0, op0=ALU.mult, op1=ALU.add,
                     )
             else:
@@ -165,10 +192,10 @@ def tile_vector_neuron_relu_k1_kernel(tc, x, w_mix, w_feat, w_dir_words, w_dir_s
         xt, xq, ub = {}, {}, {}
         uq = [mx_pair("u%d" % b, D * P) for b in range(NB)]
 
-        def turn_x(b):
+        def turn_x(b, parts=((0, 1), (2,))):
             xt[b] = work.tile([P, D, P, 4], BF16, name="xt", bufs=3, align_bytes=64)
             words = x_sb[b][:].bitcast(F32)
-            for js in ((0, 1), (2,)):
+            for js in parts:
                 bank = next_bank()
                 for i, j in enumerate(js):
                     for u in range(2):
@@ -184,13 +211,18 @@ def tile_vector_neuron_relu_k1_kernel(tc, x, w_mix, w_feat, w_dir_words, w_dir_s
             quantize(xq[b], slice(0, 256), flat[:, 0:1024])
             quantize(xq[b], slice(256, 384), flat[:, 1024:1536])
 
+        def quant_x1(b, j):
+            if j == 0:
+                xq[b] = mx_pair("xq", D * P, work)
+            quantize(xq[b], slice(P * j, P * (j + 1)), xt[b][:, j].rearrange("p n t -> p (n t)"))
+
         def mix(b, j):
             if j == 0:
                 ub[b] = work.tile([P, D, P, 4], BF16, name="ub", align_bytes=64)
             bank = next_bank()
             for t in range(4):
                 mm(bank[:, P * t : P * (t + 1)], fp8(wm, P * t, P * (t + 1)), fp8(xq[b], P * j, P * (j + 1)))
-            if b >= MIXG:
+            if MIXE[D * b + j] == "G":
                 part = work.tile([P, P, 4], F32, name="part", bufs=3)
                 nc.scalar.copy(out=part[:], in_=bank[:].rearrange("p (t n) -> p n t", t=4))
                 nc.gpsimd.tensor_tensor(out=ub[b][:, j], in0=part[:], in1=xt[b][:, j], op=ALU.add)
@@ -240,7 +272,12 @@ def tile_vector_neuron_relu_k1_kernel(tc, x, w_mix, w_feat, w_dir_words, w_dir_s
 
         def coef(k, total):
             cc[k] = work.tile([P, P, 4], F32, name="cc")
-            nc.vector.scalar_tensor_tensor(out=cc[k][:], in0=total, scalar=0.0, in1=rr[k][:], op0=ALU.min, op1=ALU.mult)
+            if CG[k] == "G":
+                neg = work.tile([P, P, 4], F32, name="neg")
+                nc.scalar.activation(out=neg[:], in_=total, func=ACT.Relu, scale=-1.0)
+                nc.gpsimd.tensor_tensor(out=cc[k][:], in0=neg[:], in1=rr[k][:], op=ALU.mult)
+            else:
+                nc.vector.scalar_tensor_tensor(out=cc[k][:], in0=total, scalar=0.0, in1=rr[k][:], op0=ALU.min, op1=ALU.mult)
 
         def along(k, j):
             b, g = divmod(k, NG)
@@ -256,7 +293,7 @@ def tile_vector_neuron_relu_k1_kernel(tc, x, w_mix, w_feat, w_dir_words, w_dir_s
             for t in range(4):
                 mm(bank[:, P * t : P * (t + 1)], fp8(wf[g], P * t, P * (t + 1)), fp8(uq[b], P * j, P * (j + 1)))
             hb[k, j] = work.tile([P, P, 4], BF16, name="hb", bufs=4, align_bytes=64)
-            nc.vector.tensor_tensor(out=hb[k, j][:], in0=bank[:].rearrange("p (t n) -> p n t", t=4), in1=mv[k, j][:], op=ALU.subtract)
+            nc.vector.tensor_tensor(out=hb[k, j][:], in0=bank[:].rearrange("p (t n) -> p n t", t=4), in1=mv[k, j][:], op=ALU.add if CG[k] == "G" else ALU.subtract)
 
         def quant_h(k, j):
             hq[k, j] = mx_pair("hq", P, work, bufs=12)
@@ -286,9 +323,40 @@ def tile_vector_neuron_relu_k1_kernel(tc, x, w_mix, w_feat, w_dir_words, w_dir_s
             elif h == 1:
                 nc.sync.dma_start(out=out_0[j, P * b : P * (b + 1), :], in_=ys[b, j][:])
 
+        def outs_both(b, j):
+            ys[b, j] = work.tile([P, N], F32, name="ys", bufs=3)
+            yb[b, j] = work.tile([P, N], BF16, name="yb", bufs=4)
+            banks = []
+            for h in range(2):
+                bank = next_bank()
+                banks.append(bank)
+                for g in range(NG):
+                    mm(bank[:], fp8(hq[NG * b + g, j], 0, P), fp8(wo[g], 512 * h, 512 * (h + 1)), start=(g == 0), stop=(g == NG - 1))
+            for h in range(2):
+                nc.vector.tensor_copy(
+                    out=yb[b, j][:, 512 * h : 512 * (h + 1)].rearrange("n (u p e) -> n u p e", u=2, e=2),
+                    in_=banks[h][:].rearrange("n (p u e) -> n u p e", u=2, e=2),
+                )
+                o = 1 - h
+                nc.scalar.copy(out=ys[b, j][:, 512 * o : 512 * (o + 1)], in_=banks[o][:])
+                nc.sync.dma_start(out=out_0[j, P * b : P * (b + 1), 512 * o : 512 * (o + 1)], in_=ys[b, j][:, 512 * o : 512 * (o + 1)])
+
+        def turn_y2(b, j):
+            words = yb[b, j][:].bitcast(F32)
+            yt[b, j] = work.tile([P, NG * 512], BF16, name="yt", bufs=4, align_bytes=64)
+            for g in range(NG):
+                bank = next_bank()
+                for u in range(2):
+                    nc.tensor.transpose(bank[:, P * u : P * (u + 1)], words[:, P * (2 * g + u) : P * (2 * g + u + 1)], ident[:])
+                move = nc.scalar.copy if g == 0 else nc.vector.tensor_copy
+                move(
+                    out=yt[b, j][:, 512 * g : 512 * (g + 1)].bitcast(F32).rearrange("p (n u) -> p n u", u=2),
+                    in_=bank[:, 0:256].rearrange("p (u n) -> p n u", u=2),
+                )
+
         def round_y(b, j, h, CONV=CONV):
-            dst = yb[b, j][:, 512 * h : 512 * (h + 1)].rearrange("n (u p e) -> n p u e", u=2, e=2)
-            src = ys[b, j][:, 512 * h : 512 * (h + 1)].rearrange("n (p u e) -> n p u e", u=2, e=2)
+            dst = yb[b, j][:, 512 * h : 512 * (h + 1)].rearrange("n (u p e) -> n u p e", u=2, e=2)
+            src = ys[b, j][:, 512 * h : 512 * (h + 1)].rearrange("n (p u e) -> n u p e", u=2, e=2)
             if CONV == "V":
                 nc.vector.tensor_copy(out=dst, in_=src)
             if CONV == "G":
@@ -323,22 +391,43 @@ def tile_vector_neuron_relu_k1_kernel(tc, x, w_mix, w_feat, w_dir_words, w_dir_s
                 )
 
         NK = NB * NG
-        group_wm()
-        turn_x(0)
-        turn_x(1)
-        quantize(wm, slice(0, C), grouped["wm"][:])
-        quant_x(0)
-        group_wf(0)
-        permute_wd()
-        quant_x(1)
-        mix(0, 0)
-        mix(0, 1)
-        quant_u(0, 0)
-        mix(0, 2)
-        quant_u(0, 1)
-        quantize(wf[0], slice(0, 512), grouped["wf", 0][:])
-        quant_u(0, 2)
-        group_wf(1)
+        def hstep(tok):
+            name, j = tok[:2], int(tok[2:] or 0)
+            if name == "wp":
+                warm_pe(WARM[j])
+            if name == "gm":
+                group_wm()
+            if name == "qm":
+                quantize(wm, slice(0, C), grouped["wm"][:])
+            if name == "tx":
+                turn_x(j, ((0,), (1,), (2,)) if j == 0 else ((0, 1), (2,)))
+            if name == "qx":
+                quant_x1(0, j)
+            if name == "qX":
+                quant_x(1)
+            if name == "gf":
+                group_wf(j)
+            if name == "qf":
+                quantize(wf[j], slice(0, 512), grouped["wf", j][:])
+            if name == "pw":
+                permute_wd()
+            if name == "mx":
+                mix(0, j)
+            if name == "qu":
+                quant_u(0, j)
+            if name == "mX":
+                mix(1, j)
+            if name == "qU":
+                quant_u(1, j)
+            if name == "di":
+                dirs(0, j)
+            if name == "pr":
+                prods(0, j)
+            if name == "dI":
+                dirs(1, 0)
+
+        for tok in HEAD.split():
+            hstep(tok)
         wo_jobs = [(0, 0), (0, 1), (1, 0), (1, 1), (0, 2), (0, 3), (1, 2), (1, 3)]
         wo_quants, rows, rounds, turns, quants = [], [], [], [], []
 
@@ -352,124 +441,93 @@ def tile_vector_neuron_relu_k1_kernel(tc, x, w_mix, w_feat, w_dir_words, w_dir_s
                 if job[1] % 2 == 1:
                     wo_quants.append((job[0], job[1] // 2))
 
-        for j in range(D):
-            dirs(0, j)
-            prods(0, j)
-            if j == 0:
-                quantize(wf[1], slice(0, 512), grouped["wf", 1][:])
-        dirs(1, 0)
-        for j in range(D):
-            mix(1, j)
-        for j in range(D):
-            quant_u(1, j)
-
-        def side(k, i):
-            if i in YQ[k] and rows:
-                b, j = rows.pop(0)
+        def step(k, tok):
+            name, j = tok[0], int(tok[1:] or 0)
+            newu = k % 2 == 1 and (k + 3) // 2 < NB
+            if name == "N":
+                norm(k)
+            if name == "T":
+                while turns:
+                    job = turns.pop(0)
+                    turn_y(*job)
+                    quants.append(job)
+            if name == "X" and k % 2 == 0 and k // 2 + 2 < NB:
+                turn_x(k // 2 + 2)
+            if name == "C":
+                coef(k, dot_sum(k))
+            if name == "p":
+                prods(k + 1, j)
+            if name == "d":
+                dirs(k + 1, j)
+            if name == "D" and k + 2 < NK:
+                dirs(k + 2, 0)
+            if name == "m":
+                along(k, j)
+            if name == "h":
+                hidden(k, j)
+            if name == "M" and newu:
+                mix((k + 3) // 2, j)
+            if name == "y" and j < YQ[k]:
+                b, i = rows.pop(0)
                 for h in range(2):
-                    outs(b, j, h)
-                    if CONV == "G":
-                        round_y(b, j, h)
-                rounds.append((b, j))
-            if k % 2 == 1 and (k + 3) // 2 < NB and i in MIXAT:
-                mix((k + 3) // 2, MIXAT.index(i))
-            if i in WOAT:
+                    outs(b, i, h)
+                    round_y(b, i, h)
+                rounds.append((b, i))
+            if name == "w":
                 wo_step()
-
-        def window(k):
-            quant_h(k, 0) if not (QH_EARLY and not (k % 2 == 1 and (k + 3) // 2 < NB)) else None
-            quant_h(k, 1)
-            while quants:
-                quant_y(*quants.pop(0))
-            if k % 2 == 1 and (k + 3) // 2 < NB:
-                for j in range(D):
-                    quant_u((k + 3) // 2, j)
-            quant_h(k, 2)
-            if k % 2 == 1:
-                rows.extend((k // 2, j) for j in range(D))
-            if k % 2 == 0 and k // 2 + 2 < NB:
+            if name == "H":
+                quant_h(k, j)
+            if name == "q":
+                while quants:
+                    quant_y(*quants.pop(0))
+            if name == "u" and newu:
+                for i in range(D):
+                    quant_u((k + 3) // 2, i)
+            if name == "x" and k % 2 == 0 and k // 2 + 2 < NB:
                 quant_x(k // 2 + 2)
-            while wo_quants:
-                quant_wo(*wo_quants.pop(0))
-            while rounds:
-                b, j = rounds.pop(0)
-                if CONV == "V":
-                    round_y(b, j, 0)
-                    round_y(b, j, 1)
-                turns.append((b, j))
+            if name == "W":
+                while wo_quants:
+                    quant_wo(*wo_quants.pop())
 
         for k in range(NK - 1):
-            first_a, first_p = dirs, prods
-            if not NORM_LAST:
-                norm(k)
-            while turns:
-                job = turns.pop(0)
-                turn_y(*job)
-                quants.append(job)
-            if k % 2 == 0 and k // 2 + 2 < NB:
-                turn_x(k // 2 + 2)
-            if NORM_LAST:
-                norm(k)
-            coef(k, dot_sum(k))
-            first_p(k + 1, 0)
-            side(k, 0)
-            along(k, 0)
-            first_a(k + 1, 1)
-            first_p(k + 1, 1)
-            hidden(k, 0)
-            side(k, 1)
-            along(k, 1)
-            first_a(k + 1, 2)
-            first_p(k + 1, 2)
-            side(k, 2)
-            hidden(k, 1)
-            side(k, 3)
-            along(k, 2)
-            side(k, 4)
-            quant_h(k, 0) if QH_EARLY and not (k % 2 == 1 and (k + 3) // 2 < NB) else None
-            side(k, 6)
-            hidden(k, 2)
-            if k + 2 < NK:
-                dirs(k + 2, 0)
-            side(k, 5)
-            window(k)
+            for tok in ROUND[k % 2].split():
+                step(k, tok)
+            if k % 2 == 1:
+                rows.extend((k // 2, j) for j in range(D))
+            turns.extend(rounds)
+            rounds.clear()
         k = NK - 1
         b = NB - 1
-        norm(k)
-        for job in turns:
-            turn_y(*job)
-        coef(k, dot_sum(k))
-        for job in turns[:1]:
-            quant_y(*job)
-        along(k, 0)
-        along(k, 1)
-        hidden(k, 0)
-        along(k, 2)
-        quant_h(k, 0)
-        hidden(k, 1)
-        for job in turns[1:2]:
-            quant_y(*job)
-        hidden(k, 2)
-        quant_h(k, 1)
-        outs(b, 0, 0)
-        outs(b, 0, 1)
-        for job in turns[2:]:
-            quant_y(*job)
-        quant_h(k, 2)
-        outs(b, 1, 0, TE[0])
-        round_y(b, 0, 0, "V")
-        outs(b, 1, 1, TE[1])
-        round_y(b, 0, 1, "V")
-        outs(b, 2, 0, TE[2])
-        outs(b, 2, 1, TE[3])
-        turn_y(b, 0, TE[4])
-        round_y(b, 1, 0, "V")
-        round_y(b, 1, 1, "V")
-        turn_y(b, 1, TE[5])
-        round_y(b, 2, 0, "V")
-        round_y(b, 2, 1, "V")
-        quant_y(b, 0)
-        turn_y(b, 2, TE[6])
-        quant_y(b, 1)
-        quant_y(b, 2)
+
+        def tstep(tok):
+            name, j = tok[0], int(tok[1:2] or 0)
+            if name == "N":
+                norm(k)
+            if name == "C":
+                coef(k, dot_sum(k))
+            if name == "t" and j < len(turns):
+                turn_y(*turns[j])
+            if name == "q" and j < len(turns):
+                quant_y(*turns[j])
+            if name == "m":
+                along(k, j)
+            if name == "h":
+                hidden(k, j)
+            if name == "H":
+                quant_h(k, j)
+            if name == "o":
+                outs(b, j, int(tok[2]), tok[3])
+            if name == "r":
+                round_y(b, j, int(tok[2]), tok[3])
+            if name == "O":
+                outs_both(b, j)
+            if name == "T":
+                turn_y(b, j, tok[2])
+            if name == "U":
+                turn_y2(b, j)
+            if name == "Q":
+                quant_y(b, j)
+
+        for tok in TAIL.split():
+            tstep(tok)
         store_scales()

@@ -35,11 +35,13 @@ WARMS = True
 WMV = 4
 WFV = (0, 4)
 LOADS = "m x0 x1 f0 d s f1 o0 o1 x2 x3"
-HEAD = "wp0 gm tx0 wp1 qm qx0 qx1 qx2 tx1 gf0 pw qX mx0 mx1 qu0 mx2 qu1 qf0 qu2 gf1 di0 pr0 qf1 di1 pr1 di2 pr2 dI mX0 mX1 mX2 qU0 qU1 qU2"
-TAIL = "N t0 t1 t2 C q0 m0 m1 h0 m2 H0 h1 q1 h2 H1 o00S o01S q2 H2 o10V r00V o11S r01V o20S o21S T0S r10V r11V T1S r20V r21V Q0 T2S Q1 Q2"
-MIXE = "VVVVVVVVVVVV"
+HEAD = "wp0 gm tx0 wp1 qm qx0 qx1 qx2 tx1 gf0 pw qX mx0 mx1 qu0 mx2 qu1 qf0 qu2 gf1 di0 pr0 qf1 di1 pr1 di2 pr2 dI mX0 mX1 mX2 qU0 qU2"
+TAIL = "N C t0 t1 t2 m0 m1 h0 m2 H0 h1 a2 o00S o01S h2 H1 q0 o10S o11S H2 q1 q2 R0 o20V o21S T0S R1 T1S R2 Q0 T2S Q1 Q2"
+MIXE = "VVVVVVGVGGGG"
 CG = "VVVVVVVV"
-ROUND = ("N T X C p0 y0 w w m0 d1 p1 h0 y1 m1 d2 p2 y2 w m2 h1 h2 D w H0 H1 q H2 x W", "N T X C p0 w w m0 d1 p1 h0 y0 m1 d2 p2 w M0 m2 h1 M1 M2 h2 D w H0 H1 q u H2 W")
+ROUND = ("N T X C p0 L d1 w w m0 p1 y0 d2 h0 m1 p2 y1 y2 w m2 h1 h2 D w q u x H W", "N T X C p0 M0 d1 w w m0 p1 M1 d2 h0 m1 y0 p2 w m2 h1 M2 h2 D w q u H W")
+LATE = True
+RG = "SSSSSSSS"
 
 
 def tile_vector_neuron_relu_k1_kernel(tc, x, w_mix, w_feat, w_dir_words, w_dir_scales, w_out, out_0, out_1, out_2):
@@ -229,8 +231,8 @@ def tile_vector_neuron_relu_k1_kernel(tc, x, w_mix, w_feat, w_dir_words, w_dir_s
             else:
                 nc.vector.tensor_tensor(out=ub[b][:, j], in0=bank[:].rearrange("p (t n) -> p n t", t=4), in1=xt[b][:, j], op=ALU.add)
 
-        def quant_u(b, j):
-            quantize(uq[b], slice(P * j, P * (j + 1)), ub[b][:, j].rearrange("p n t -> p (n t)"))
+        def quant_u(b, j, n=1):
+            quantize(uq[b], slice(P * j, P * (j + n)), ub[b][:, j : j + n].rearrange("p j n t -> p (j n t)"))
 
         vs, sq, pr, rr, cc, mv, hb = {}, {}, {}, {}, {}, {}, {}
         hq = {}
@@ -265,7 +267,10 @@ def tile_vector_neuron_relu_k1_kernel(tc, x, w_mix, w_feat, w_dir_words, w_dir_s
             root = work.tile([P, P, 4], F32, name="root")
             rr[k] = work.tile([P, P, 4], F32, name="rr")
             nc.scalar.activation(out=root[:], in_=total, func=ACT.Abs_reciprocal_sqrt, bias=EPS)
-            nc.scalar.activation(out=rr[k][:], in_=root[:], func=ACT.Square)
+            if RG[k] == "G":
+                nc.gpsimd.tensor_tensor(out=rr[k][:], in0=root[:], in1=root[:], op=ALU.mult)
+            else:
+                nc.scalar.activation(out=rr[k][:], in_=root[:], func=ACT.Square)
 
         def dot_sum(k):
             return sum_turned([pr[k, j] for j in range(D)])
@@ -287,17 +292,28 @@ def tile_vector_neuron_relu_k1_kernel(tc, x, w_mix, w_feat, w_dir_words, w_dir_s
             mv[k, j] = work.tile([P, P, 4], F32, name="mv", bufs=3)
             nc.vector.tensor_tensor(out=mv[k, j][:], in0=bank[:].rearrange("p (t n) -> p n t", t=4), in1=cc[k][:], op=ALU.mult)
 
-        def hidden(k, j):
+        pre = {}
+
+        def feats(k, j):
             b, g = divmod(k, NG)
             bank = next_bank()
             for t in range(4):
                 mm(bank[:, P * t : P * (t + 1)], fp8(wf[g], P * t, P * (t + 1)), fp8(uq[b], P * j, P * (j + 1)))
-            hb[k, j] = work.tile([P, P, 4], BF16, name="hb", bufs=4, align_bytes=64)
-            nc.vector.tensor_tensor(out=hb[k, j][:], in0=bank[:].rearrange("p (t n) -> p n t", t=4), in1=mv[k, j][:], op=ALU.add if CG[k] == "G" else ALU.subtract)
+            pre[k, j] = bank
 
-        def quant_h(k, j):
-            hq[k, j] = mx_pair("hq", P, work, bufs=12)
-            quantize(hq[k, j], slice(0, P), hb[k, j][:].rearrange("p n t -> p (n t)"))
+        def hidden(k, j):
+            b, g = divmod(k, NG)
+            if (k, j) not in pre:
+                feats(k, j)
+            bank = pre[k, j]
+            if g == 0 and j == 0:
+                hb[b] = work.tile([P, NG * D * 512], BF16, name="hb", bufs=2, align_bytes=64)
+                hq[b] = mx_pair("hq", NG * D * P, work, bufs=2)
+            i = D * g + j
+            nc.vector.tensor_tensor(out=hb[b][:, 512 * i : 512 * (i + 1)].rearrange("p (n t) -> p n t", t=4), in0=bank[:].rearrange("p (t n) -> p n t", t=4), in1=mv[k, j][:], op=ALU.add if CG[k] == "G" else ALU.subtract)
+
+        def quant_h(b, lo, hi):
+            quantize(hq[b], slice(P * lo, P * hi), hb[b][:, 512 * lo : 512 * hi])
 
         ys, yb, yt = {}, {}, {}
         y_scales = keep.tile([P, NG, D * PTS], U8, name="y_scales", align_bytes=64)
@@ -308,7 +324,7 @@ def tile_vector_neuron_relu_k1_kernel(tc, x, w_mix, w_feat, w_dir_words, w_dir_s
                 yb[b, j] = work.tile([P, N], BF16, name="yb", bufs=4)
             bank = next_bank()
             for g in range(NG):
-                mm(bank[:], fp8(hq[NG * b + g, j], 0, P), fp8(wo[g], 512 * h, 512 * (h + 1)), start=(g == 0), stop=(g == NG - 1))
+                mm(bank[:], fp8(hq[b], P * (D * g + j), P * (D * g + j + 1)), fp8(wo[g], 512 * h, 512 * (h + 1)), start=(g == 0), stop=(g == NG - 1))
             if eng == "S":
                 nc.scalar.copy(out=ys[b, j][:, 512 * h : 512 * (h + 1)], in_=bank[:])
             else:
@@ -331,7 +347,7 @@ def tile_vector_neuron_relu_k1_kernel(tc, x, w_mix, w_feat, w_dir_words, w_dir_s
                 bank = next_bank()
                 banks.append(bank)
                 for g in range(NG):
-                    mm(bank[:], fp8(hq[NG * b + g, j], 0, P), fp8(wo[g], 512 * h, 512 * (h + 1)), start=(g == 0), stop=(g == NG - 1))
+                    mm(bank[:], fp8(hq[b], P * (D * g + j), P * (D * g + j + 1)), fp8(wo[g], 512 * h, 512 * (h + 1)), start=(g == 0), stop=(g == NG - 1))
             for h in range(2):
                 nc.vector.tensor_copy(
                     out=yb[b, j][:, 512 * h : 512 * (h + 1)].rearrange("n (u p e) -> n u p e", u=2, e=2),
@@ -353,6 +369,12 @@ def tile_vector_neuron_relu_k1_kernel(tc, x, w_mix, w_feat, w_dir_words, w_dir_s
                     out=yt[b, j][:, 512 * g : 512 * (g + 1)].bitcast(F32).rearrange("p (n u) -> p n u", u=2),
                     in_=bank[:, 0:256].rearrange("p (u n) -> p n u", u=2),
                 )
+
+        def round_row(b, j):
+            nc.vector.tensor_copy(
+                out=yb[b, j][:].rearrange("n (g u p e) -> n g u p e", g=NG, u=2, e=2),
+                in_=ys[b, j][:].rearrange("n (g p u e) -> n g u p e", g=NG, u=2, e=2),
+            )
 
         def round_y(b, j, h, CONV=CONV):
             dst = yb[b, j][:, 512 * h : 512 * (h + 1)].rearrange("n (u p e) -> n u p e", u=2, e=2)
@@ -418,7 +440,7 @@ def tile_vector_neuron_relu_k1_kernel(tc, x, w_mix, w_feat, w_dir_words, w_dir_s
             if name == "mX":
                 mix(1, j)
             if name == "qU":
-                quant_u(1, j)
+                quant_u(1, j, 2 if j == 0 else 1)
             if name == "di":
                 dirs(0, j)
             if name == "pr":
@@ -465,7 +487,7 @@ def tile_vector_neuron_relu_k1_kernel(tc, x, w_mix, w_feat, w_dir_words, w_dir_s
                 along(k, j)
             if name == "h":
                 hidden(k, j)
-            if name == "M" and newu:
+            if name == "M" and newu and (j < 2 or not LATE):
                 mix((k + 3) // 2, j)
             if name == "y" and j < YQ[k]:
                 b, i = rows.pop(0)
@@ -475,14 +497,23 @@ def tile_vector_neuron_relu_k1_kernel(tc, x, w_mix, w_feat, w_dir_words, w_dir_s
                 rounds.append((b, i))
             if name == "w":
                 wo_step()
-            if name == "H":
-                quant_h(k, j)
+            if name == "H" and k % 2 == 0:
+                quant_h(k // 2, 0, 2)
+                if k == NK - 2:
+                    quant_h(k // 2, 2, 3)
+            if name == "H" and k % 2 == 1:
+                quant_h(k // 2, 2, 6)
+            if name == "L" and k % 2 == 0 and 2 <= k // 2 + 1 < NB and LATE:
+                mix(k // 2 + 1, 2)
             if name == "q":
                 while quants:
                     quant_y(*quants.pop(0))
             if name == "u" and newu:
-                for i in range(D):
-                    quant_u((k + 3) // 2, i)
+                quant_u((k + 3) // 2, 0, 2)
+                if not LATE:
+                    quant_u((k + 3) // 2, 2)
+            if name == "u" and k % 2 == 0 and 2 <= k // 2 + 1 < NB and LATE:
+                quant_u(k // 2 + 1, 2)
             if name == "x" and k % 2 == 0 and k // 2 + 2 < NB:
                 quant_x(k // 2 + 2)
             if name == "W":
@@ -514,7 +545,16 @@ def tile_vector_neuron_relu_k1_kernel(tc, x, w_mix, w_feat, w_dir_words, w_dir_s
             if name == "h":
                 hidden(k, j)
             if name == "H":
-                quant_h(k, j)
+                quant_h(b, D + j, D + j + 1)
+            if name == "z":
+                for h in range(2):
+                    outs(b - 1, 2, h)
+                    round_y(b - 1, 2, h, tok[2])
+                turns.append((b - 1, 2))
+            if name == "a":
+                feats(k, j)
+            if name == "R":
+                round_row(b, j)
             if name == "o":
                 outs(b, j, int(tok[2]), tok[3])
             if name == "r":

from contextlib import ExitStack

import concourse.mybir as mybir
from concourse.masks import make_identity

F32 = mybir.dt.float32
BF16 = mybir.dt.bfloat16
I32 = mybir.dt.int32
U32 = mybir.dt.uint32
U8 = mybir.dt.uint8
FP8X4 = mybir.dt.float8_e4m3fn_x4
FP4X4 = mybir.dt.float4_e2m1fn_x4
ALU = mybir.AluOpType
ACT = mybir.ActivationFunctionType

D, PTS, C, F, N = 3, 512, 512, 1024, 1024
EPS = 0.1
P = 128
NB = PTS // P
NG = F // 512
FLOPS = 2 * D * PTS * (C * C + 2 * C * F + F * N)
CONV = "G"
YQ = (0, 0, 2, 1, 2, 1, 3)
NORM_LAST = False
WO = "GGGGSSSS"
QADD = 0
MIXAT = (2, 4, 6)
WOAT = (0, 1, 2, 5)
MIXG = 4
TC = "GG"
TE = "VSSSSSS"
QH_EARLY = False
WARM = (0, 0)
WARMS = True
WMV = 4
WFV = (0, 4)
LOADS = "m x0 x1 f0 d s f1 o0 o1 x2 x3"
HEAD = "wp0 gm tx0 wp1 qm qx0 qx1 qx2 tx1 gf0 pw qX mx0 mx1 qu0 mx2 qu1 qf0 qu2 gf1 di0 pr0 qf1 di1 pr1 di2 pr2 dI mX0 mX1 mX2 qU0 qU2"
TAIL = "N C t0 t1 t2 m0 m1 h0 m2 H0 h1 a2 o00S o01S h2 H1 q0 o10S o11S H2 q1 q2 R0 o20V o21S T0S R1 T1S R2 Q0 T2S Q1 Q2"
MIXE = "VVVVVVGVGGGG"
CG = "VVVVVVVV"
ROUND = ("N T X C p0 L d1 w w m0 p1 y0 d2 h0 m1 p2 y1 y2 w m2 h1 h2 D w q u x H W", "N T X C p0 M0 d1 w w m0 p1 M1 d2 h0 m1 y0 p2 w m2 h1 M2 h2 D w q u H W")
LATE = True
RG = "SSSSSSSS"


def tile_vector_neuron_relu_k1_kernel(tc, x, w_mix, w_feat, w_dir_words, w_dir_scales, w_out, out_0, out_1, out_2):
    nc = tc.nc
    with ExitStack() as ctx:
        keep = ctx.enter_context(tc.tile_pool(name="keep", bufs=1))
        work = ctx.enter_context(tc.tile_pool(name="work", bufs=2))
        psum = ctx.enter_context(tc.psum_pool(name="psum", bufs=1))
        ctx.enter_context(tc.manual_schedule())

        taken = []

        def next_bank():
            bank = psum.tile([P, 512], F32, name="bank%d" % (len(taken) % 8))
            taken.append(bank)
            return bank

        def mx_pair(name, width, pool=keep, bufs=None):
            codes = pool.tile([P, width], U32, name=name + "_codes", align_bytes=64, bufs=bufs)
            scales = pool.tile([P, width], U8, name=name + "_scales", align_bytes=64, bufs=bufs)
            return codes, scales

        def quantize(pair, cols, src):
            nc.vector.quantize_mx(out=pair[0][:, cols].bitcast(FP8X4), scales=pair[1][:, cols], in_=src)

        def mm(out, lhs, rhs, start=True, stop=True):
            nc.tensor.matmul_mx(out=out, lhsT=lhs[0], lhsT_scale=lhs[1], rhs=rhs[0], rhs_scale=rhs[1], start=start, stop=stop)

        def fp8(pair, lo, hi):
            return pair[0][:, lo:hi].bitcast(FP8X4), pair[1][:, lo:hi]

        def fp4(pair, lo, hi):
            return pair[0][:, 2 * lo : 2 * hi].bitcast(FP4X4), pair[1][:, lo:hi]

        ident = keep.tile([P, P], F32, name="ident")
        wd_sraw = keep.tile([P, F], U8, name="wd_sraw", align_bytes=64)
        make_identity(nc, ident[:])
        nc.gpsimd.memset(wd_sraw[:].bitcast(I32), 0)
        if WARM[0]:
            ones = keep.tile([P, 512], BF16, name="ones")
            nc.vector.memset(ones[:], 1.0)
        if WARMS:
            warm = keep.tile([P, 8], F32, name="warm")
            nc.scalar.activation(out=warm[:, 0:1], in_=ident[:, 0:1], func=ACT.Abs_reciprocal_sqrt, bias=EPS)

        x_sb = [keep.tile([P, D, C], BF16, name="x%d" % b, align_bytes=64) for b in range(NB)]
        wm_raw = keep.tile([P, 4, C], BF16, name="wm_raw")
        wf_raw = [keep.tile([P, 4, 512], BF16, name="wf_raw%d" % g) for g in range(NG)]
        wo_raw = [keep.tile([P, 4, N], BF16, name="wo_raw%d" % g) for g in range(NG)]
        wd_wraw = keep.tile([P, 2 * F], U8, name="wd_wraw", align_bytes=64)

        def load_x(b):
            nc.sync.dma_start(out=x_sb[b][:], in_=x[:, P * b : P * (b + 1), :].rearrange("j p c -> p j c"))

        def load_wf(g):
            nc.sync.dma_start(out=wf_raw[g][:], in_=w_feat[:, 512 * g : 512 * (g + 1)].rearrange("(p j) n -> p j n", j=4))

        def load_wo(g):
            rows = w_out.rearrange("(g s t r) n -> g r s t n", g=NG, t=4, r=4)
            for r in range(4):
                nc.sync.dma_start(out=wo_raw[g][r:P:4, :, :], in_=rows[g, r])

        def load(tok):
            if tok == "m":
                nc.sync.dma_start(out=wm_raw[:], in_=w_mix.rearrange("(p j) n -> p j n", j=4))
            if tok == "d":
                nc.sync.dma_start(out=wd_wraw[:].bitcast(I32), in_=w_dir_words[0].bitcast(I32))
            if tok == "s":
                for q in range(4):
                    nc.sync.dma_start(out=wd_sraw[32 * q : 32 * q + 4, :].bitcast(I32), in_=w_dir_scales[0, 4 * q : 4 * q + 4, :].bitcast(I32))
            if tok[0] == "x":
                load_x(int(tok[1]))
            if tok[0] == "f":
                load_wf(int(tok[1]))
            if tok[0] == "o":
                load_wo(int(tok[1]))

        for tok in LOADS.split():
            load(tok)

        def warm_pe(n):
            if n:
                bank = next_bank()
                for i in range(n):
                    nc.tensor.matmul(bank[:], ones[:, 0:P], ones[:], start=True, stop=True)

        wm = mx_pair("wm", C)
        wf = [mx_pair("wf%d" % g, 512) for g in range(NG)]
        wo = [mx_pair("wo%d" % g, N) for g in range(NG)]
        wd = (keep.tile([P, 2 * F], U8, name="wd_codes", align_bytes=64), keep.tile([P, F], U8, name="wd_scales", align_bytes=64))
        grouped = {}

        def group_wm():
            t = work.tile([P, 2048], BF16, name="wgroup", bufs=4, align_bytes=64)
            dst = t[:].rearrange("p (t a e j) -> p a t e j", t=4, e=2, j=4)
            src = wm_raw[:].rearrange("p j (a e t) -> p a t e j", e=2, t=4)
            nc.vector.tensor_copy(out=dst[:, :, :WMV], in_=src[:, :, :WMV])
            if WMV < 4:
                nc.scalar.copy(out=dst[:, :, WMV:], in_=src[:, :, WMV:])
            grouped["wm"] = t

        def group_wf(g):
            if g == 1:
                t = work.tile([P, 2048], BF16, name="wgate", bufs=1, align_bytes=64)
            else:
                t = work.tile([P, 2048], BF16, name="wgroup", bufs=4, align_bytes=64)
            dst = t[:].rearrange("p (t s r j) -> p s t j r", t=4, r=4, j=4)
            src = wf_raw[g][:].rearrange("p j (s t r) -> p s t j r", t=4, r=4)
            if WFV[g] > 0:
                nc.vector.tensor_copy(out=dst[:, :, : WFV[g]], in_=src[:, :, : WFV[g]])
            if WFV[g] < 4:
                nc.scalar.copy(out=dst[:, :, WFV[g] :], in_=src[:, :, WFV[g] :])
            grouped["wf", g] = t

        def group_wo(g, q):
            if q % 2 == 0 and WO[4 * g + q] == "G":
                grouped["wo", g, q // 2] = work.tile([P, 2048], BF16, name="wgate", bufs=1, align_bytes=64)
            elif q % 2 == 0:
                grouped["wo", g, q // 2] = work.tile([P, 2048], BF16, name="wgroup", bufs=4, align_bytes=64)
            t = grouped["wo", g, q // 2]
            eng = WO[4 * g + q]
            if eng == "G":
                for e in range(2):
                    lo = 1024 * (q % 2) + 512 * e
                    nc.gpsimd.tensor_scalar(
                        out=t[:, lo : lo + 512].rearrange("p (n t) -> p n t", t=4),
                        in0=wo_raw[g][:, :, 256 * q + 128 * e : 256 * q + 128 * (e + 1)].rearrange("p t n -> p n t"),
                        scalar1=1.0, scalar2=0.0, op0=ALU.mult, op1=ALU.add,
                    )
            else:
                move = nc.scalar.copy if eng == "S" else nc.vector.tensor_copy
                move(
                    out=t[:, 1024 * (q % 2) : 1024 * (q % 2 + 1)].rearrange("p (c i t) -> p c t i", i=4, t=4),
                    in_=wo_raw[g][:, :, 256 * q : 256 * (q + 1)].rearrange("p t (c i) -> p c t i", i=4),
                )

        def quant_wo(g, h):
            quantize(wo[g], slice(512 * h, 512 * (h + 1)), grouped["wo", g, h][:])

        def permute_wd():
            nc.vector.tensor_copy(
                out=wd[0][:].bitcast(I32).rearrange("p (g t s h) -> p g t s h", g=NG, t=4, h=2),
                in_=wd_wraw[:].bitcast(I32).rearrange("p (g s t h) -> p g t s h", g=NG, t=4, h=2),
            )
            nc.vector.tensor_copy(
                out=wd[1][:].bitcast(I32).rearrange("p (g t s) -> p g t s", g=NG, t=4),
                in_=wd_sraw[:].bitcast(I32).rearrange("p (g s t) -> p g t s", g=NG, t=4),
            )

        xt, xq, ub = {}, {}, {}
        uq = [mx_pair("u%d" % b, D * P) for b in range(NB)]

        def turn_x(b, parts=((0, 1), (2,))):
            xt[b] = work.tile([P, D, P, 4], BF16, name="xt", bufs=3, align_bytes=64)
            words = x_sb[b][:].bitcast(F32)
            for js in parts:
                bank = next_bank()
                for i, j in enumerate(js):
                    for u in range(2):
                        nc.tensor.transpose(bank[:, P * (2 * i + u) : P * (2 * i + u + 1)], words[:, j, u:256:2], ident[:])
                nc.scalar.copy(
                    out=xt[b][:, js[0] : js[-1] + 1].rearrange("p j n t -> p (j n t)").bitcast(F32).rearrange("p (j n u) -> p j n u", n=P, u=2),
                    in_=bank[:, : 256 * len(js)].rearrange("p (j u n) -> p j n u", u=2, n=P),
                )

        def quant_x(b):
            xq[b] = mx_pair("xq", D * P, work)
            flat = xt[b][:].rearrange("p j n t -> p (j n t)")
            quantize(xq[b], slice(0, 256), flat[:, 0:1024])
            quantize(xq[b], slice(256, 384), flat[:, 1024:1536])

        def quant_x1(b, j):
            if j == 0:
                xq[b] = mx_pair("xq", D * P, work)
            quantize(xq[b], slice(P * j, P * (j + 1)), xt[b][:, j].rearrange("p n t -> p (n t)"))

        def mix(b, j):
            if j == 0:
                ub[b] = work.tile([P, D, P, 4], BF16, name="ub", align_bytes=64)
            bank = next_bank()
            for t in range(4):
                mm(bank[:, P * t : P * (t + 1)], fp8(wm, P * t, P * (t + 1)), fp8(xq[b], P * j, P * (j + 1)))
            if MIXE[D * b + j] == "G":
                part = work.tile([P, P, 4], F32, name="part", bufs=3)
                nc.scalar.copy(out=part[:], in_=bank[:].rearrange("p (t n) -> p n t", t=4))
                nc.gpsimd.tensor_tensor(out=ub[b][:, j], in0=part[:], in1=xt[b][:, j], op=ALU.add)
            else:
                nc.vector.tensor_tensor(out=ub[b][:, j], in0=bank[:].rearrange("p (t n) -> p n t", t=4), in1=xt[b][:, j], op=ALU.add)

        def quant_u(b, j, n=1):
            quantize(uq[b], slice(P * j, P * (j + n)), ub[b][:, j : j + n].rearrange("p j n t -> p (j n t)"))

        vs, sq, pr, rr, cc, mv, hb = {}, {}, {}, {}, {}, {}, {}
        hq = {}

        def dirs(k, j):
            b, g = divmod(k, NG)
            bank = next_bank()
            mm(bank[:], fp8(uq[b], P * j, P * (j + 1)), fp4(wd, 512 * g, 512 * (g + 1)))
            vs[k, j] = work.tile([P, 512], F32, name="vs", bufs=3)
            sq[k, j] = work.tile([P, 512], F32, name="sq", bufs=4)
            nc.scalar.copy(out=vs[k, j][:], in_=bank[:])
            nc.scalar.activation(out=sq[k, j][:], in_=bank[:], func=ACT.Square)
            if j >= 1 and j <= QADD:
                nc.gpsimd.tensor_tensor(out=sq[k, j][:], in0=sq[k, j][:], in1=sq[k, j - 1][:], op=ALU.add)

        def prods(k, j):
            b, g = divmod(k, NG)
            bank = next_bank()
            mm(bank[:], fp8(uq[b], P * j, P * (j + 1)), fp8(wf[g], 0, 512))
            pr[k, j] = work.tile([P, 512], F32, name="pr", bufs=4)
            nc.vector.tensor_tensor(out=pr[k, j][:], in0=bank[:], in1=vs[k, j][:], op=ALU.mult)

        def sum_turned(terms):
            bank = next_bank()
            for t in range(4):
                for j in range(len(terms)):
                    nc.tensor.matmul(bank[:, P * t : P * (t + 1)], terms[j][:, P * t : P * (t + 1)], ident[:], start=(j == 0), stop=(j == len(terms) - 1), is_transpose=True)
            return bank[:].rearrange("p (t n) -> p n t", t=4)

        def norm(k):
            total = sum_turned([sq[k, j] for j in range(QADD, D)])
            root = work.tile([P, P, 4], F32, name="root")
            rr[k] = work.tile([P, P, 4], F32, name="rr")
            nc.scalar.activation(out=root[:], in_=total, func=ACT.Abs_reciprocal_sqrt, bias=EPS)
            if RG[k] == "G":
                nc.gpsimd.tensor_tensor(out=rr[k][:], in0=root[:], in1=root[:], op=ALU.mult)
            else:
                nc.scalar.activation(out=rr[k][:], in_=root[:], func=ACT.Square)

        def dot_sum(k):
            return sum_turned([pr[k, j] for j in range(D)])

        def coef(k, total):
            cc[k] = work.tile([P, P, 4], F32, name="cc")
            if CG[k] == "G":
                neg = work.tile([P, P, 4], F32, name="neg")
                nc.scalar.activation(out=neg[:], in_=total, func=ACT.Relu, scale=-1.0)
                nc.gpsimd.tensor_tensor(out=cc[k][:], in0=neg[:], in1=rr[k][:], op=ALU.mult)
            else:
                nc.vector.scalar_tensor_tensor(out=cc[k][:], in0=total, scalar=0.0, in1=rr[k][:], op0=ALU.min, op1=ALU.mult)

        def along(k, j):
            b, g = divmod(k, NG)
            bank = next_bank()
            for t in range(4):
                mm(bank[:, P * t : P * (t + 1)], fp4(wd, 512 * g + P * t, 512 * g + P * (t + 1)), fp8(uq[b], P * j, P * (j + 1)))
            mv[k, j] = work.tile([P, P, 4], F32, name="mv", bufs=3)
            nc.vector.tensor_tensor(out=mv[k, j][:], in0=bank[:].rearrange("p (t n) -> p n t", t=4), in1=cc[k][:], op=ALU.mult)

        pre = {}

        def feats(k, j):
            b, g = divmod(k, NG)
            bank = next_bank()
            for t in range(4):
                mm(bank[:, P * t : P * (t + 1)], fp8(wf[g], P * t, P * (t + 1)), fp8(uq[b], P * j, P * (j + 1)))
            pre[k, j] = bank

        def hidden(k, j):
            b, g = divmod(k, NG)
            if (k, j) not in pre:
                feats(k, j)
            bank = pre[k, j]
            if g == 0 and j == 0:
                hb[b] = work.tile([P, NG * D * 512], BF16, name="hb", bufs=2, align_bytes=64)
                hq[b] = mx_pair("hq", NG * D * P, work, bufs=2)
            i = D * g + j
            nc.vector.tensor_tensor(out=hb[b][:, 512 * i : 512 * (i + 1)].rearrange("p (n t) -> p n t", t=4), in0=bank[:].rearrange("p (t n) -> p n t", t=4), in1=mv[k, j][:], op=ALU.add if CG[k] == "G" else ALU.subtract)

        def quant_h(b, lo, hi):
            quantize(hq[b], slice(P * lo, P * hi), hb[b][:, 512 * lo : 512 * hi])

        ys, yb, yt = {}, {}, {}
        y_scales = keep.tile([P, NG, D * PTS], U8, name="y_scales", align_bytes=64)

        def outs(b, j, h, eng="S"):
            if h == 0:
                ys[b, j] = work.tile([P, N], F32, name="ys", bufs=3)
                yb[b, j] = work.tile([P, N], BF16, name="yb", bufs=4)
            bank = next_bank()
            for g in range(NG):
                mm(bank[:], fp8(hq[b], P * (D * g + j), P * (D * g + j + 1)), fp8(wo[g], 512 * h, 512 * (h + 1)), start=(g == 0), stop=(g == NG - 1))
            if eng == "S":
                nc.scalar.copy(out=ys[b, j][:, 512 * h : 512 * (h + 1)], in_=bank[:])
            else:
                nc.vector.tensor_copy(out=ys[b, j][:, 512 * h : 512 * (h + 1)], in_=bank[:])
            if CONV == "S":
                nc.scalar.copy(
                    out=yb[b, j][:, 512 * h : 512 * (h + 1)].rearrange("n (u p e) -> n u p e", u=2, e=2),
                    in_=bank[:].rearrange("n (p u e) -> n u p e", u=2, e=2),
                )
            if b == NB - 1:
                nc.sync.dma_start(out=out_0[j, P * b : P * (b + 1), 512 * h : 512 * (h + 1)], in_=ys[b, j][:, 512 * h : 512 * (h + 1)])
            elif h == 1:
                nc.sync.dma_start(out=out_0[j, P * b : P * (b + 1), :], in_=ys[b, j][:])

        def outs_both(b, j):
            ys[b, j] = work.tile([P, N], F32, name="ys", bufs=3)
            yb[b, j] = work.tile([P, N], BF16, name="yb", bufs=4)
            banks = []
            for h in range(2):
                bank = next_bank()
                banks.append(bank)
                for g in range(NG):
                    mm(bank[:], fp8(hq[b], P * (D * g + j), P * (D * g + j + 1)), fp8(wo[g], 512 * h, 512 * (h + 1)), start=(g == 0), stop=(g == NG - 1))
            for h in range(2):
                nc.vector.tensor_copy(
                    out=yb[b, j][:, 512 * h : 512 * (h + 1)].rearrange("n (u p e) -> n u p e", u=2, e=2),
                    in_=banks[h][:].rearrange("n (p u e) -> n u p e", u=2, e=2),
                )
                o = 1 - h
                nc.scalar.copy(out=ys[b, j][:, 512 * o : 512 * (o + 1)], in_=banks[o][:])
                nc.sync.dma_start(out=out_0[j, P * b : P * (b + 1), 512 * o : 512 * (o + 1)], in_=ys[b, j][:, 512 * o : 512 * (o + 1)])

        def turn_y2(b, j):
            words = yb[b, j][:].bitcast(F32)
            yt[b, j] = work.tile([P, NG * 512], BF16, name="yt", bufs=4, align_bytes=64)
            for g in range(NG):
                bank = next_bank()
                for u in range(2):
                    nc.tensor.transpose(bank[:, P * u : P * (u + 1)], words[:, P * (2 * g + u) : P * (2 * g + u + 1)], ident[:])
                move = nc.scalar.copy if g == 0 else nc.vector.tensor_copy
                move(
                    out=yt[b, j][:, 512 * g : 512 * (g + 1)].bitcast(F32).rearrange("p (n u) -> p n u", u=2),
                    in_=bank[:, 0:256].rearrange("p (u n) -> p n u", u=2),
                )

        def round_row(b, j):
            nc.vector.tensor_copy(
                out=yb[b, j][:].rearrange("n (g u p e) -> n g u p e", g=NG, u=2, e=2),
                in_=ys[b, j][:].rearrange("n (g p u e) -> n g u p e", g=NG, u=2, e=2),
            )

        def round_y(b, j, h, CONV=CONV):
            dst = yb[b, j][:, 512 * h : 512 * (h + 1)].rearrange("n (u p e) -> n u p e", u=2, e=2)
            src = ys[b, j][:, 512 * h : 512 * (h + 1)].rearrange("n (p u e) -> n u p e", u=2, e=2)
            if CONV == "V":
                nc.vector.tensor_copy(out=dst, in_=src)
            if CONV == "G":
                nc.gpsimd.tensor_scalar(out=dst, in0=src, scalar1=1.0, scalar2=0.0, op0=ALU.mult, op1=ALU.add)

        def turn_y(b, j, eng="S"):
            bank = next_bank()
            words = yb[b, j][:].bitcast(F32)
            for i in range(4):
                nc.tensor.transpose(bank[:, P * i : P * (i + 1)], words[:, P * i : P * (i + 1)], ident[:])
            yt[b, j] = work.tile([P, NG * 512], BF16, name="yt", bufs=4, align_bytes=64)
            move = nc.scalar.copy if eng == "S" else nc.vector.tensor_copy
            move(
                out=yt[b, j][:].bitcast(F32).rearrange("p (g n u) -> p g n u", g=NG, u=2),
                in_=bank[:].rearrange("p (g u n) -> p g n u", g=NG, u=2),
            )

        def quant_y(b, j):
            cols = slice(PTS * j + P * b, PTS * j + P * (b + 1))
            y_codes = work.tile([P, NG, P], U32, name="y_codes", bufs=6, align_bytes=64)
            for g in range(NG):
                nc.vector.quantize_mx(out=y_codes[:, g, :].bitcast(FP8X4), scales=y_scales[:, g, cols], in_=yt[b, j][:, 512 * g : 512 * (g + 1)])
            dst = out_1.rearrange("g p m t -> p g (m t)").bitcast(I32)
            nc.sync.dma_start(out=dst[:, :, cols], in_=y_codes[:].bitcast(I32))

        def store_scales():
            for q in range(4):
                queue = nc.sync if q % 2 == 0 else nc.scalar
                queue.dma_start(
                    out=out_2[:, 4 * q : 4 * q + 4, :].rearrange("g r m -> r g m").bitcast(I32),
                    in_=y_scales[32 * q : 32 * q + 4, :, :].bitcast(I32),
                )

        NK = NB * NG
        def hstep(tok):
            name, j = tok[:2], int(tok[2:] or 0)
            if name == "wp":
                warm_pe(WARM[j])
            if name == "gm":
                group_wm()
            if name == "qm":
                quantize(wm, slice(0, C), grouped["wm"][:])
            if name == "tx":
                turn_x(j, ((0,), (1,), (2,)) if j == 0 else ((0, 1), (2,)))
            if name == "qx":
                quant_x1(0, j)
            if name == "qX":
                quant_x(1)
            if name == "gf":
                group_wf(j)
            if name == "qf":
                quantize(wf[j], slice(0, 512), grouped["wf", j][:])
            if name == "pw":
                permute_wd()
            if name == "mx":
                mix(0, j)
            if name == "qu":
                quant_u(0, j)
            if name == "mX":
                mix(1, j)
            if name == "qU":
                quant_u(1, j, 2 if j == 0 else 1)
            if name == "di":
                dirs(0, j)
            if name == "pr":
                prods(0, j)
            if name == "dI":
                dirs(1, 0)

        for tok in HEAD.split():
            hstep(tok)
        wo_jobs = [(0, 0), (0, 1), (1, 0), (1, 1), (0, 2), (0, 3), (1, 2), (1, 3)]
        wo_quants, rows, rounds, turns, quants = [], [], [], [], []

        def skip(*args):
            return None

        def wo_step():
            if wo_jobs:
                job = wo_jobs.pop(0)
                group_wo(*job)
                if job[1] % 2 == 1:
                    wo_quants.append((job[0], job[1] // 2))

        def step(k, tok):
            name, j = tok[0], int(tok[1:] or 0)
            newu = k % 2 == 1 and (k + 3) // 2 < NB
            if name == "N":
                norm(k)
            if name == "T":
                while turns:
                    job = turns.pop(0)
                    turn_y(*job)
                    quants.append(job)
            if name == "X" and k % 2 == 0 and k // 2 + 2 < NB:
                turn_x(k // 2 + 2)
            if name == "C":
                coef(k, dot_sum(k))
            if name == "p":
                prods(k + 1, j)
            if name == "d":
                dirs(k + 1, j)
            if name == "D" and k + 2 < NK:
                dirs(k + 2, 0)
            if name == "m":
                along(k, j)
            if name == "h":
                hidden(k, j)
            if name == "M" and newu and (j < 2 or not LATE):
                mix((k + 3) // 2, j)
            if name == "y" and j < YQ[k]:
                b, i = rows.pop(0)
                for h in range(2):
                    outs(b, i, h)
                    round_y(b, i, h)
                rounds.append((b, i))
            if name == "w":
                wo_step()
            if name == "H" and k % 2 == 0:
                quant_h(k // 2, 0, 2)
                if k == NK - 2:
                    quant_h(k // 2, 2, 3)
            if name == "H" and k % 2 == 1:
                quant_h(k // 2, 2, 6)
            if name == "L" and k % 2 == 0 and 2 <= k // 2 + 1 < NB and LATE:
                mix(k // 2 + 1, 2)
            if name == "q":
                while quants:
                    quant_y(*quants.pop(0))
            if name == "u" and newu:
                quant_u((k + 3) // 2, 0, 2)
                if not LATE:
                    quant_u((k + 3) // 2, 2)
            if name == "u" and k % 2 == 0 and 2 <= k // 2 + 1 < NB and LATE:
                quant_u(k // 2 + 1, 2)
            if name == "x" and k % 2 == 0 and k // 2 + 2 < NB:
                quant_x(k // 2 + 2)
            if name == "W":
                while wo_quants:
                    quant_wo(*wo_quants.pop())

        for k in range(NK - 1):
            for tok in ROUND[k % 2].split():
                step(k, tok)
            if k % 2 == 1:
                rows.extend((k // 2, j) for j in range(D))
            turns.extend(rounds)
            rounds.clear()
        k = NK - 1
        b = NB - 1

        def tstep(tok):
            name, j = tok[0], int(tok[1:2] or 0)
            if name == "N":
                norm(k)
            if name == "C":
                coef(k, dot_sum(k))
            if name == "t" and j < len(turns):
                turn_y(*turns[j])
            if name == "q" and j < len(turns):
                quant_y(*turns[j])
            if name == "m":
                along(k, j)
            if name == "h":
                hidden(k, j)
            if name == "H":
                quant_h(b, D + j, D + j + 1)
            if name == "z":
                for h in range(2):
                    outs(b - 1, 2, h)
                    round_y(b - 1, 2, h, tok[2])
                turns.append((b - 1, 2))
            if name == "a":
                feats(k, j)
            if name == "R":
                round_row(b, j)
            if name == "o":
                outs(b, j, int(tok[2]), tok[3])
            if name == "r":
                round_y(b, j, int(tok[2]), tok[3])
            if name == "O":
                outs_both(b, j)
            if name == "T":
                turn_y(b, j, tok[2])
            if name == "U":
                turn_y2(b, j)
            if name == "Q":
                quant_y(b, j)

        for tok in TAIL.split():
            tstep(tok)
        store_scales()
